import numpy as np, ml_dtypes
CORES = [21,29,37,45,53,61,69,77,85]
N = 9
B, S = 16, 64
def entries(a): return a.T.reshape(-1)
def pack(v, P): return np.ascontiguousarray(np.asarray(v, np.int32).reshape(-1, P).T)
def lists(rng, how):
    Q = rng.integers(0, N * B, N * B)
    if how == "alike": Q[:] = rng.integers(N * B)
    if how == "stay": Q = np.arange(N * B)
    if how == "distinct": Q = rng.permutation(N * B)
    if how == "hotrank": Q = B * int(rng.integers(N)) + rng.integers(0, B, N * B)
    if how == "swap": s = int(rng.integers(1, N)); Q = np.concatenate([B * ((r + s) % N) + rng.permutation(B) for r in range(N)])
    return {"parent": np.broadcast_to(pack(Q, 16), (N, 16, N * B // 16)).copy()}
def setup_inputs(rng):
    return dict({"c": rng.standard_normal((N, 128, B * S), dtype=np.float32).astype(ml_dtypes.bfloat16)}, **lists(rng, "uniform"))
def setup_inputs_alike(rng):
    d = setup_inputs(rng); d.update(lists(rng, "alike"))
    for k in ("c",): d[k] = (d[k].astype(np.float32) * 1048576.0).astype(d[k].dtype)
    return d
def setup_inputs_distinct(rng):
    d = setup_inputs(rng); d.update(lists(rng, "distinct"))
    for k in ("c",): d[k] = (d[k].astype(np.float32) * (1 / 1024.0)).astype(d[k].dtype)
    return d
def setup_inputs_hotrank(rng):
    d = setup_inputs(rng); d.update(lists(rng, "hotrank"))
    return d
def setup_inputs_stay(rng):
    d = setup_inputs(rng); d.update(lists(rng, "stay"))
    return d
def setup_inputs_swap(rng):
    d = setup_inputs(rng); d.update(lists(rng, "swap"))
    return d
def check_inputs(x):
    bad = []
    if x["parent"].min() < 0 or x["parent"].max() >= N * B: bad.append("parent out of range")
    if not all(np.array_equal(a, x["parent"][0]) for a in x["parent"]): bad.append("parent isn't alike on all ranks")
    return bad
def reference(c, parent):
    A = np.concatenate(list(c), axis=1).reshape(128, N * B, S)
    Y = A[:, entries(parent[0]), :]
    return {"y": np.stack([Y[:, B * r:B * r + B].reshape(128, B * S) for r in range(N)])}

@@ -1,0 +1,181 @@
+from concourse.bass import DstId, RemoteDMATransfer
+from concourse.mybir import AluOpType, ActivationFunctionType
+
+N, B, S = 9, 16, 64
+W = 4
+M = S // W
+BW = B * W
+
+SCRATCH = {
+    "csb": ("sbuf", [128, B, M, W], "bfloat16"),
+    "snd": ("sbuf", [128, M * BW], "bfloat16"),
+    "hb": ("sbuf", [128, (M // 4) * BW], "bfloat16"),
+    "win": ("sbuf", [128, N * BW], "bfloat16"),
+    "par": ("sbuf", [128, N], "int32"),
+    "off": ("sbuf", [128, N * W], "uint16"),
+    "offl": ("sbuf", [128, N * W], "uint16"),
+    "gat": ("sbuf", [128, N * BW], "bfloat16"),
+    "land": ("sbuf", [128, M * BW], "bfloat16"),
+    "ysb": ("sbuf", [128, B * S], "bfloat16"),
+}
+SEMAPHORES = ["c", "par", "off", "rl", "loc", "hb", "win", "offl", "gat", "land", "y", "st"]
+
+
+def _engs(mask):
+    return [i for i in range(mask.bit_length()) if (mask >> i) & 1]
+
+
+def _pow2(n):
+    p = 1
+    while p * 2 <= n:
+        p *= 2
+    return p
+
+
+def _split(topo, src, dsts):
+    far = [d for d in dsts if topo.chip(d) != topo.chip(src)]
+    near = [d for d in dsts if topo.chip(d) == topo.chip(src)]
+    out, used = {}, []
+    if far:
+        used = _engs(topo.mask(src, far[0]))
+        n = _pow2(len(used) // len(far))
+        for i, d in enumerate(far):
+            out[d] = used[i * n:(i + 1) * n]
+    if near:
+        rest = [e for e in _engs(topo.mask(src, near[0])) if e not in used]
+        n = _pow2(len(rest) // len(near))
+        for i, d in enumerate(near):
+            out[d] = rest[i * n:(i + 1) * n]
+    return out
+
+
+def _plan(T, topo):
+    cores = list(T.cores)
+    allc = range(topo.CORES_PER_CHIP * topo.CHIPS)
+    chips = [topo.chip(c) for c in cores]
+    ports = {}
+    for ch in chips:
+        mate = [o for o in range(topo.CHIPS) if topo.mates(ch, o)][0]
+        far = [c for c in allc if topo.chip(c) == mate][0]
+        by_die = {}
+        for c in allc:
+            if topo.chip(c) == ch and c not in cores and topo.may_write(c, far):
+                by_die.setdefault(topo.die(c), []).append(c)
+        ports[ch] = by_die
+    dies = sorted(ports[chips[0]])
+    per = M // len(dies)
+    keeper, die_of = [], []
+    for k, x in enumerate(dies):
+        for j in range(per):
+            keeper.append(ports[chips[k * (N - per) + j]][x][0])
+            die_of.append(x)
+    carry = []
+    for r in range(N):
+        lst = []
+        for x in dies:
+            a, b = ports[chips[r]][x][:2]
+            mine = [m for m in range(M) if die_of[m] == x]
+            mine = [m for m in mine if keeper[m] != a] + [m for m in mine if keeper[m] == a]
+            lst.append((a, mine[:per // 2]))
+            lst.append((b, mine[per // 2:]))
+        carry.append(lst)
+    return cores, keeper, carry
+
+
+def _send(g, topo, src, items, local_sem):
+    eng = _split(topo, src, [it[0] for it in items])
+    total = 0
+    for away in (True, False):
+        trs = []
+        for dst, sap, dap, rsem in items:
+            if (topo.chip(dst) != topo.chip(src)) != away:
+                continue
+            rid, pid, _se = topo.addr(dst)
+            trs.append(RemoteDMATransfer(dst_ids=[DstId(rid=rid, pnc=pid)],
+                                         dma_engine_mask=sum(1 << e for e in eng[dst]),
+                                         remote_sem=rsem, src=sap, dst=dap))
+            total += len(eng[dst])
+        if trs:
+            g.remote_dma_fused(trs, local_sem=local_sem)
+    return total
+
+
+def rank_program(g, core, T, topo):
+    cores, keeper, carry = _plan(T, topo)
+    sem = T.sem
+    rank = T.rank_of(core)
+    copy = ActivationFunctionType.Copy
+    sent = 0
+
+    if rank is not None:
+        g.sync.dma_start(T.csb[:, :, :, :], T.c[:, :]).then_inc(sem.c, 16)
+        here = [k for k in keeper if topo.chip(k) == topo.chip(core)]
+        if here:
+            for k in range(128 // B):
+                g.scalar.dma_start(T.par[B * k:B * (k + 1), :], T.parent[:, :]).then_inc(sem.par, 16)
+            g.vector.wait_ge(sem.par, 16 * (128 // B))
+            for e in range(W):
+                g.vector.tensor_scalar(T.off[:, e:N * W:W], T.par[:, :], W, e,
+                                       AluOpType.mult, AluOpType.add).then_inc(sem.off, 1)
+            g.wait_ge(sem.off, W)
+            sent += _send(g, topo, core, [(k, T.off[:, :], T.offl[:, :], sem.offl) for k in here], sem.loc)
+        g.vector.wait_ge(sem.c, 16)
+        g.scalar.wait_ge(sem.c, 16)
+        slot = 0
+        items = []
+        for h, ms in carry[rank]:
+            items.append((h, T.snd[:, slot * BW:(slot + len(ms)) * BW], T.hb[:, :], sem.hb))
+            for m in ms:
+                out, in_ = T.snd[:, slot * BW:(slot + 1) * BW], T.csb[:, :, m, :]
+                if slot % 2 == 0:
+                    g.vector.tensor_copy(out, in_).then_inc(sem.rl, 1)
+                else:
+                    g.scalar.activation(out, in_, copy).then_inc(sem.rl, 1)
+                slot += 1
+        g.wait_ge(sem.rl, M)
+        sent += _send(g, topo, core, items, sem.loc)
+        want = sum(len(_split(topo, k, cores)[core]) for k in keeper)
+        g.vector.wait_ge(sem.land, want)
+        g.scalar.wait_ge(sem.land, want)
+        for q in range(B):
+            out, in_ = T.ysb[:, q * S:(q + 1) * S], T.land[:, q:M * BW:B]
+            if q % 2 == 0:
+                g.vector.tensor_copy(out, in_).then_inc(sem.y, 1)
+            else:
+                g.scalar.activation(out, in_, copy).then_inc(sem.y, 1)
+        g.sync.wait_ge(sem.y, B)
+        g.sync.dma_start(T.y[:, :], T.ysb[:, :]).then_inc(sem.st, 16)
+        g.wait_ge(sem.loc, sent)
+        g.sync.wait_ge(sem.st, 16)
+        return
+
+    mine = [(r, ms) for r in range(N) for h, ms in carry[r] if h == core]
+    if not mine:
+        return
+    r, ms = mine[0]
+    g.wait_ge(sem.hb, len(_split(topo, cores[r], [h for h, _m in carry[r]])[core]))
+    sent += _send(g, topo, core,
+                  [(keeper[m], T.hb[:, i * BW:(i + 1) * BW], T.win[:, r * BW:(r + 1) * BW], sem.win)
+                   for i, m in enumerate(ms)], sem.loc)
+    if core in keeper:
+        m = keeper.index(core)
+        want = 0
+        for rr in range(N):
+            for h, hms in carry[rr]:
+                if m in hms:
+                    want += len(_split(topo, h, [keeper[x] for x in hms])[core])
+        here = [k for k in keeper if topo.chip(k) == topo.chip(core)]
+        noff = len(_split(topo, cores[r], here)[core])
+        for q in (g.vector, g.scalar):
+            q.wait_ge(sem.offl, noff)
+            q.wait_ge(sem.win, want)
+        a = (N + 1) // 2
+        g.vector.tensor_copy(T.gat[:, 0:a * BW],
+                             T.win[:, 0:N * BW].indirect(T.offl[:, 0:a * W])).then_inc(sem.gat, 1)
+        g.scalar.activation(T.gat[:, a * BW:N * BW],
+                            T.win[:, 0:N * BW].indirect(T.offl[:, a * W:N * W]), copy).then_inc(sem.gat, 1)
+        g.wait_ge(sem.gat, 2)
+        sent += _send(g, topo, core,
+                      [(cores[d], T.gat[:, d * BW:(d + 1) * BW], T.land[:, m * BW:(m + 1) * BW], sem.land)
+                       for d in range(N)], sem.loc)
+    g.wait_ge(sem.loc, sent)

@@ -12,13 +12,13 @@ SCRATCH = {
     "hb": ("sbuf", [128, (M // 4) * BW], "bfloat16"),
     "win": ("sbuf", [128, N * BW], "bfloat16"),
     "par": ("sbuf", [128, N], "int32"),
-    "off": ("sbuf", [128, N * W], "uint16"),
+    "parl": ("sbuf", [128, N], "int32"),
     "offl": ("sbuf", [128, N * W], "uint16"),
     "gat": ("sbuf", [128, N * BW], "bfloat16"),
     "land": ("sbuf", [128, M * BW], "bfloat16"),
     "ysb": ("sbuf", [128, B * S], "bfloat16"),
 }
-SEMAPHORES = ["c", "par", "off", "rl", "loc", "hb", "win", "offl", "gat", "land", "y", "st"]
+SEMAPHORES = ["c", "par", "off", "rl0", "rl1", "loc", "hb", "win", "parl", "gat", "land", "y0", "y1", "st"]
 
 
 def _engs(mask):
@@ -32,15 +32,18 @@ def _pow2(n):
     return p
 
 
-def _split(topo, src, dsts):
+def _split(topo, src, dsts, together=False):
     far = [d for d in dsts if topo.chip(d) != topo.chip(src)]
     near = [d for d in dsts if topo.chip(d) == topo.chip(src)]
     out, used = {}, []
     if far:
         used = _engs(topo.mask(src, far[0]))
-        n = _pow2(len(used) // len(far))
-        for i, d in enumerate(far):
+        grp = far + near if together else far
+        n = _pow2(len(used) // len(grp))
+        for i, d in enumerate(grp):
             out[d] = used[i * n:(i + 1) * n]
+        if together:
+            return out
     if near:
         rest = [e for e in _engs(topo.mask(src, near[0])) if e not in used]
         n = _pow2(len(rest) // len(near))
@@ -72,7 +75,7 @@ def _plan(T, topo):
     carry = []
     for r in range(N):
         lst = []
-        for x in dies:
+        for x in sorted(dies, key=lambda d: d == topo.die(cores[r])):
             a, b = ports[chips[r]][x][:2]
             mine = [m for m in range(M) if die_of[m] == x]
             mine = [m for m in mine if keeper[m] != a] + [m for m in mine if keeper[m] == a]
@@ -82,13 +85,13 @@ def _plan(T, topo):
     return cores, keeper, carry
 
 
-def _send(g, topo, src, items, local_sem):
-    eng = _split(topo, src, [it[0] for it in items])
+def _send(g, topo, src, items, local_sem, together=False):
+    eng = _split(topo, src, [it[0] for it in items], together)
     total = 0
     for away in (True, False):
         trs = []
         for dst, sap, dap, rsem in items:
-            if (topo.chip(dst) != topo.chip(src)) != away:
+            if not together and (topo.chip(dst) != topo.chip(src)) != away:
                 continue
             rid, pid, _se = topo.addr(dst)
             trs.append(RemoteDMATransfer(dst_ids=[DstId(rid=rid, pnc=pid)],
@@ -97,6 +100,8 @@ def _send(g, topo, src, items, local_sem):
             total += len(eng[dst])
         if trs:
             g.remote_dma_fused(trs, local_sem=local_sem)
+        if together:
+            break
     return total
 
 
@@ -110,64 +115,71 @@ def rank_program(g, core, T, topo):
     if rank is not None:
         g.sync.dma_start(T.csb[:, :, :, :], T.c[:, :]).then_inc(sem.c, 16)
         here = [k for k in keeper if topo.chip(k) == topo.chip(core)]
-        if here:
-            for k in range(128 // B):
-                g.scalar.dma_start(T.par[B * k:B * (k + 1), :], T.parent[:, :]).then_inc(sem.par, 16)
-            g.vector.wait_ge(sem.par, 16 * (128 // B))
-            for e in range(W):
-                g.vector.tensor_scalar(T.off[:, e:N * W:W], T.par[:, :], W, e,
-                                       AluOpType.mult, AluOpType.add).then_inc(sem.off, 1)
-            g.wait_ge(sem.off, W)
-            sent += _send(g, topo, core, [(k, T.off[:, :], T.offl[:, :], sem.offl) for k in here], sem.loc)
+        for k in range(128 // B):
+            q = g.scalar if k % 2 == 0 else g.sync
+            q.dma_start(T.par[B * k:B * (k + 1), :], T.parent[:, :]).then_inc(sem.par, 16)
+        g.wait_ge(sem.par, 16 * (128 // B))
+        sent += _send(g, topo, core, [(k, T.par[:, :], T.parl[:, :], sem.parl) for k in here], sem.loc)
         g.vector.wait_ge(sem.c, 16)
         g.scalar.wait_ge(sem.c, 16)
         slot = 0
-        items = []
-        for h, ms in carry[rank]:
-            items.append((h, T.snd[:, slot * BW:(slot + len(ms)) * BW], T.hb[:, :], sem.hb))
-            for m in ms:
-                out, in_ = T.snd[:, slot * BW:(slot + 1) * BW], T.csb[:, :, m, :]
-                if slot % 2 == 0:
-                    g.vector.tensor_copy(out, in_).then_inc(sem.rl, 1)
-                else:
-                    g.scalar.activation(out, in_, copy).then_inc(sem.rl, 1)
-                slot += 1
-        g.wait_ge(sem.rl, M)
-        sent += _send(g, topo, core, items, sem.loc)
+        for half in range(2):
+            rl = sem["rl%d" % half]
+            items = []
+            for h, ms in carry[rank][2 * half:2 * half + 2]:
+                items.append((h, T.snd[:, slot * BW:(slot + len(ms)) * BW], T.hb[:, :], sem.hb))
+                for m in ms:
+                    out, in_ = T.snd[:, slot * BW:(slot + 1) * BW], T.csb[:, :, m, :]
+                    if slot % 2 == 0:
+                        g.vector.tensor_copy(out, in_).then_inc(rl, 1)
+                    else:
+                        g.scalar.activation(out, in_, copy).then_inc(rl, 1)
+                    slot += 1
+            g.wait_ge(rl, M // 2)
+            sent += _send(g, topo, core, items, sem.loc)
         want = sum(len(_split(topo, k, cores)[core]) for k in keeper)
         g.vector.wait_ge(sem.land, want)
         g.scalar.wait_ge(sem.land, want)
-        for q in range(B):
-            out, in_ = T.ysb[:, q * S:(q + 1) * S], T.land[:, q:M * BW:B]
-            if q % 2 == 0:
-                g.vector.tensor_copy(out, in_).then_inc(sem.y, 1)
-            else:
-                g.scalar.activation(out, in_, copy).then_inc(sem.y, 1)
-        g.sync.wait_ge(sem.y, B)
-        g.sync.dma_start(T.y[:, :], T.ysb[:, :]).then_inc(sem.st, 16)
+        for half in range(2):
+            ys = sem["y%d" % half]
+            for q in range(half * B // 2, (half + 1) * B // 2):
+                out, in_ = T.ysb[:, q * S:(q + 1) * S], T.land[:, q:M * BW:B]
+                if q % 2 == 0:
+                    g.vector.tensor_copy(out, in_).then_inc(ys, 1)
+                else:
+                    g.scalar.activation(out, in_, copy).then_inc(ys, 1)
+            lo, hi = half * B * S // 2, (half + 1) * B * S // 2
+            g.sync.wait_ge(ys, B // 2)
+            g.sync.dma_start(T.y[:, lo:hi], T.ysb[:, lo:hi]).then_inc(sem.st, 16)
         g.wait_ge(sem.loc, sent)
-        g.sync.wait_ge(sem.st, 16)
+        g.sync.wait_ge(sem.st, 32)
         return
 
-    mine = [(r, ms) for r in range(N) for h, ms in carry[r] if h == core]
+    mine = [(r, i, ms) for r in range(N) for i, (h, ms) in enumerate(carry[r]) if h == core]
     if not mine:
         return
-    r, ms = mine[0]
-    g.wait_ge(sem.hb, len(_split(topo, cores[r], [h for h, _m in carry[r]])[core]))
+    r, i, ms = mine[0]
+    pair = [h for h, _m in carry[r][i - i % 2:i - i % 2 + 2]]
+    is_keeper = core in keeper
+    if is_keeper:
+        here = [k for k in keeper if topo.chip(k) == topo.chip(core)]
+        g.vector.wait_ge(sem.parl, len(_split(topo, cores[r], here)[core]))
+        for e in range(W):
+            g.vector.tensor_scalar(T.offl[:, e:N * W:W], T.parl[:, :], W, e,
+                                   AluOpType.mult, AluOpType.add).then_inc(sem.off, 1)
+    g.wait_ge(sem.hb, len(_split(topo, cores[r], pair)[core]))
     sent += _send(g, topo, core,
-                  [(keeper[m], T.hb[:, i * BW:(i + 1) * BW], T.win[:, r * BW:(r + 1) * BW], sem.win)
-                   for i, m in enumerate(ms)], sem.loc)
-    if core in keeper:
+                  [(keeper[m], T.hb[:, j * BW:(j + 1) * BW], T.win[:, r * BW:(r + 1) * BW], sem.win)
+                   for j, m in enumerate(ms)], sem.loc, together=True)
+    if is_keeper:
         m = keeper.index(core)
         want = 0
         for rr in range(N):
             for h, hms in carry[rr]:
                 if m in hms:
-                    want += len(_split(topo, h, [keeper[x] for x in hms])[core])
-        here = [k for k in keeper if topo.chip(k) == topo.chip(core)]
-        noff = len(_split(topo, cores[r], here)[core])
+                    want += len(_split(topo, h, [keeper[x] for x in hms], True)[core])
         for q in (g.vector, g.scalar):
-            q.wait_ge(sem.offl, noff)
+            q.wait_ge(sem.off, W)
             q.wait_ge(sem.win, want)
         a = (N + 1) // 2
         g.vector.tensor_copy(T.gat[:, 0:a * BW],

@@ -5,6 +5,8 @@ N, B, S = 9, 16, 64
 W = 4
 M = S // W
 BW = B * W
+Q = 2 * B
+H = (N - 1) // 2
 
 SCRATCH = {
     "csb": ("sbuf", [128, B, M, W], "bfloat16"),
@@ -18,7 +20,8 @@ SCRATCH = {
     "land": ("sbuf", [128, M * BW], "bfloat16"),
     "ysb": ("sbuf", [128, B * S], "bfloat16"),
 }
-SEMAPHORES = ["c", "par", "off", "rl0", "rl1", "loc", "hb", "win", "parl", "gat", "land", "y0", "y1", "st"]
+SEMAPHORES = ["c", "par", "ms", "rep", "off", "rl0", "rl1", "loc", "hb", "win", "parl", "g0", "g1", "land",
+              "y0", "y1", "st"]
 
 
 def _engs(mask):
@@ -85,6 +88,10 @@ def _plan(T, topo):
     return cores, keeper, carry
 
 
+def _order(r):
+    return [(r + 1 + i) % N for i in range(N)]
+
+
 def _send(g, topo, src, items, local_sem, together=False):
     eng = _split(topo, src, [it[0] for it in items], together)
     total = 0
@@ -113,12 +120,14 @@ def rank_program(g, core, T, topo):
     sent = 0
 
     if rank is not None:
-        g.sync.dma_start(T.csb[:, :, :, :], T.c[:, :]).then_inc(sem.c, 16)
         here = [k for k in keeper if topo.chip(k) == topo.chip(core)]
-        for k in range(128 // B):
-            q = g.scalar if k % 2 == 0 else g.sync
-            q.dma_start(T.par[B * k:B * (k + 1), :], T.parent[:, :]).then_inc(sem.par, 16)
-        g.wait_ge(sem.par, 16 * (128 // B))
+        g.sync.dma_start(T.par[0:B, :], T.parent[:, :]).then_inc(sem.par, 16)
+        g.scalar.dma_start(T.par[B:Q, :], T.parent[:, :]).then_inc(sem.par, 16)
+        g.sync.dma_start(T.csb[:, :, :, :], T.c[:, :]).then_inc(sem.c, 16)
+        g.vector.memset(T.par[Q:2 * Q, :], 0).then_inc(sem.ms, 1)
+        g.vector.memset(T.par[2 * Q:128, :], 0).then_inc(sem.ms, 1)
+        g.wait_ge(sem.par, 32)
+        g.wait_ge(sem.ms, 2)
         sent += _send(g, topo, core, [(k, T.par[:, :], T.parl[:, :], sem.parl) for k in here], sem.loc)
         g.vector.wait_ge(sem.c, 16)
         g.scalar.wait_ge(sem.c, 16)
@@ -137,7 +146,11 @@ def rank_program(g, core, T, topo):
                     slot += 1
             g.wait_ge(rl, M // 2)
             sent += _send(g, topo, core, items, sem.loc)
-        want = sum(len(_split(topo, k, cores)[core]) for k in keeper)
+        want = 0
+        for k in keeper:
+            o = _order([r for r in range(N) if topo.chip(cores[r]) == topo.chip(k)][0])
+            wave = o[:H] if rank in o[:H] else o[H:]
+            want += len(_split(topo, k, [cores[d] for d in wave])[core])
         g.vector.wait_ge(sem.land, want)
         g.scalar.wait_ge(sem.land, want)
         for half in range(2):
@@ -161,12 +174,25 @@ def rank_program(g, core, T, topo):
     r, i, ms = mine[0]
     pair = [h for h, _m in carry[r][i - i % 2:i - i % 2 + 2]]
     is_keeper = core in keeper
+    noff = 0
     if is_keeper:
         here = [k for k in keeper if topo.chip(k) == topo.chip(core)]
-        g.vector.wait_ge(sem.parl, len(_split(topo, cores[r], here)[core]))
+        got = len(_split(topo, cores[r], here)[core])
+        for q in (g.sync, g.scalar, g.vector):
+            q.wait_ge(sem.parl, got)
+        for j in range(1, 128 // Q):
+            q = g.sync if j % 2 else g.scalar
+            q.dma_start(T.parl[j * Q:(j + 1) * Q, :], T.parl[0:Q, :]).then_inc(sem.rep, 16)
+        g.vector.wait_ge(sem.rep, 16 * (128 // Q - 1))
+        n1 = N - 1 - r
         for e in range(W):
-            g.vector.tensor_scalar(T.offl[:, e:N * W:W], T.parl[:, :], W, e,
+            if n1:
+                g.vector.tensor_scalar(T.offl[:, e:n1 * W:W], T.parl[:, r + 1:N], W, e,
+                                       AluOpType.mult, AluOpType.add).then_inc(sem.off, 1)
+                noff += 1
+            g.vector.tensor_scalar(T.offl[:, n1 * W + e:N * W:W], T.parl[:, 0:r + 1], W, e,
                                    AluOpType.mult, AluOpType.add).then_inc(sem.off, 1)
+            noff += 1
     g.wait_ge(sem.hb, len(_split(topo, cores[r], pair)[core]))
     sent += _send(g, topo, core,
                   [(keeper[m], T.hb[:, j * BW:(j + 1) * BW], T.win[:, r * BW:(r + 1) * BW], sem.win)
@@ -179,15 +205,20 @@ def rank_program(g, core, T, topo):
                 if m in hms:
                     want += len(_split(topo, h, [keeper[x] for x in hms], True)[core])
         for q in (g.vector, g.scalar):
-            q.wait_ge(sem.off, W)
+            q.wait_ge(sem.off, noff)
             q.wait_ge(sem.win, want)
-        a = (N + 1) // 2
-        g.vector.tensor_copy(T.gat[:, 0:a * BW],
-                             T.win[:, 0:N * BW].indirect(T.offl[:, 0:a * W])).then_inc(sem.gat, 1)
-        g.scalar.activation(T.gat[:, a * BW:N * BW],
-                            T.win[:, 0:N * BW].indirect(T.offl[:, a * W:N * W]), copy).then_inc(sem.gat, 1)
-        g.wait_ge(sem.gat, 2)
-        sent += _send(g, topo, core,
-                      [(cores[d], T.gat[:, d * BW:(d + 1) * BW], T.land[:, m * BW:(m + 1) * BW], sem.land)
-                       for d in range(N)], sem.loc)
+        order = _order(r)
+        waves = [(0, H), (H, N)]
+        for w, (lo, hi) in enumerate(waves):
+            a, z = lo * W, hi * W
+            mid = (a + z) // 2
+            g.vector.tensor_copy(T.gat[:, a * B:mid * B],
+                                 T.win[:, 0:N * BW].indirect(T.offl[:, a:mid])).then_inc(sem["g%d" % w], 1)
+            g.scalar.activation(T.gat[:, mid * B:z * B],
+                                T.win[:, 0:N * BW].indirect(T.offl[:, mid:z]), copy).then_inc(sem["g%d" % w], 1)
+        for w, (lo, hi) in enumerate(waves):
+            g.wait_ge(sem["g%d" % w], 2)
+            sent += _send(g, topo, core,
+                          [(cores[order[p]], T.gat[:, p * BW:(p + 1) * BW], T.land[:, m * BW:(m + 1) * BW], sem.land)
+                           for p in range(lo, hi)], sem.loc)
     g.wait_ge(sem.loc, sent)

from concourse.bass import DstId, RemoteDMATransfer
from concourse.mybir import AluOpType, ActivationFunctionType

N, B, S = 9, 16, 64
W = 4
M = S // W
BW = B * W
Q = 2 * B
H = (N - 1) // 2

SCRATCH = {
    "csb": ("sbuf", [128, B, M, W], "bfloat16"),
    "snd": ("sbuf", [128, M * BW], "bfloat16"),
    "hb": ("sbuf", [128, (M // 4) * BW], "bfloat16"),
    "win": ("sbuf", [128, N * BW], "bfloat16"),
    "par": ("sbuf", [128, N], "int32"),
    "parl": ("sbuf", [128, N], "int32"),
    "offl": ("sbuf", [128, N * W], "uint16"),
    "gat": ("sbuf", [128, N * BW], "bfloat16"),
    "land": ("sbuf", [128, M * BW], "bfloat16"),
    "ysb": ("sbuf", [128, B * S], "bfloat16"),
}
SEMAPHORES = ["c", "par", "ms", "rep", "off", "rl0", "rl1", "loc", "hb", "win", "parl", "g0", "g1", "land",
              "y0", "y1", "st"]


def _engs(mask):
    return [i for i in range(mask.bit_length()) if (mask >> i) & 1]


def _pow2(n):
    p = 1
    while p * 2 <= n:
        p *= 2
    return p


def _split(topo, src, dsts, together=False):
    far = [d for d in dsts if topo.chip(d) != topo.chip(src)]
    near = [d for d in dsts if topo.chip(d) == topo.chip(src)]
    out, used = {}, []
    if far:
        used = _engs(topo.mask(src, far[0]))
        grp = far + near if together else far
        n = _pow2(len(used) // len(grp))
        for i, d in enumerate(grp):
            out[d] = used[i * n:(i + 1) * n]
        if together:
            return out
    if near:
        rest = [e for e in _engs(topo.mask(src, near[0])) if e not in used]
        n = _pow2(len(rest) // len(near))
        for i, d in enumerate(near):
            out[d] = rest[i * n:(i + 1) * n]
    return out


def _plan(T, topo):
    cores = list(T.cores)
    allc = range(topo.CORES_PER_CHIP * topo.CHIPS)
    chips = [topo.chip(c) for c in cores]
    ports = {}
    for ch in chips:
        mate = [o for o in range(topo.CHIPS) if topo.mates(ch, o)][0]
        far = [c for c in allc if topo.chip(c) == mate][0]
        by_die = {}
        for c in allc:
            if topo.chip(c) == ch and c not in cores and topo.may_write(c, far):
                by_die.setdefault(topo.die(c), []).append(c)
        ports[ch] = by_die
    dies = sorted(ports[chips[0]])
    per = M // len(dies)
    keeper, die_of = [], []
    for k, x in enumerate(dies):
        for j in range(per):
            keeper.append(ports[chips[k * (N - per) + j]][x][0])
            die_of.append(x)
    carry = []
    for r in range(N):
        lst = []
        for x in sorted(dies, key=lambda d: d == topo.die(cores[r])):
            a, b = ports[chips[r]][x][:2]
            mine = [m for m in range(M) if die_of[m] == x]
            mine = [m for m in mine if keeper[m] != a] + [m for m in mine if keeper[m] == a]
            lst.append((a, mine[:per // 2]))
            lst.append((b, mine[per // 2:]))
        carry.append(lst)
    return cores, keeper, carry


def _order(r):
    return [(r + 1 + i) % N for i in range(N)]


def _send(g, topo, src, items, local_sem, together=False):
    eng = _split(topo, src, [it[0] for it in items], together)
    total = 0
    for away in (True, False):
        trs = []
        for dst, sap, dap, rsem in items:
            if not together and (topo.chip(dst) != topo.chip(src)) != away:
                continue
            rid, pid, _se = topo.addr(dst)
            trs.append(RemoteDMATransfer(dst_ids=[DstId(rid=rid, pnc=pid)],
                                         dma_engine_mask=sum(1 << e for e in eng[dst]),
                                         remote_sem=rsem, src=sap, dst=dap))
            total += len(eng[dst])
        if trs:
            g.remote_dma_fused(trs, local_sem=local_sem)
        if together:
            break
    return total


def rank_program(g, core, T, topo):
    cores, keeper, carry = _plan(T, topo)
    sem = T.sem
    rank = T.rank_of(core)
    copy = ActivationFunctionType.Copy
    sent = 0

    if rank is not None:
        here = [k for k in keeper if topo.chip(k) == topo.chip(core)]
        g.sync.dma_start(T.par[0:B, :], T.parent[:, :]).then_inc(sem.par, 16)
        g.scalar.dma_start(T.par[B:Q, :], T.parent[:, :]).then_inc(sem.par, 16)
        g.sync.dma_start(T.csb[:, :, :, :], T.c[:, :]).then_inc(sem.c, 16)
        g.vector.memset(T.par[Q:2 * Q, :], 0).then_inc(sem.ms, 1)
        g.vector.memset(T.par[2 * Q:128, :], 0).then_inc(sem.ms, 1)
        g.wait_ge(sem.par, 32)
        g.wait_ge(sem.ms, 2)
        sent += _send(g, topo, core, [(k, T.par[:, :], T.parl[:, :], sem.parl) for k in here], sem.loc)
        g.vector.wait_ge(sem.c, 16)
        g.scalar.wait_ge(sem.c, 16)
        slot = 0
        for half in range(2):
            rl = sem["rl%d" % half]
            items = []
            for h, ms in carry[rank][2 * half:2 * half + 2]:
                items.append((h, T.snd[:, slot * BW:(slot + len(ms)) * BW], T.hb[:, :], sem.hb))
                for m in ms:
                    out, in_ = T.snd[:, slot * BW:(slot + 1) * BW], T.csb[:, :, m, :]
                    if slot % 2 == 0:
                        g.vector.tensor_copy(out, in_).then_inc(rl, 1)
                    else:
                        g.scalar.activation(out, in_, copy).then_inc(rl, 1)
                    slot += 1
            g.wait_ge(rl, M // 2)
            sent += _send(g, topo, core, items, sem.loc)
        want = 0
        for k in keeper:
            o = _order([r for r in range(N) if topo.chip(cores[r]) == topo.chip(k)][0])
            wave = o[:H] if rank in o[:H] else o[H:]
            want += len(_split(topo, k, [cores[d] for d in wave])[core])
        g.vector.wait_ge(sem.land, want)
        g.scalar.wait_ge(sem.land, want)
        for half in range(2):
            ys = sem["y%d" % half]
            for q in range(half * B // 2, (half + 1) * B // 2):
                out, in_ = T.ysb[:, q * S:(q + 1) * S], T.land[:, q:M * BW:B]
                if q % 2 == 0:
                    g.vector.tensor_copy(out, in_).then_inc(ys, 1)
                else:
                    g.scalar.activation(out, in_, copy).then_inc(ys, 1)
            lo, hi = half * B * S // 2, (half + 1) * B * S // 2
            g.sync.wait_ge(ys, B // 2)
            g.sync.dma_start(T.y[:, lo:hi], T.ysb[:, lo:hi]).then_inc(sem.st, 16)
        g.wait_ge(sem.loc, sent)
        g.sync.wait_ge(sem.st, 32)
        return

    mine = [(r, i, ms) for r in range(N) for i, (h, ms) in enumerate(carry[r]) if h == core]
    if not mine:
        return
    r, i, ms = mine[0]
    pair = [h for h, _m in carry[r][i - i % 2:i - i % 2 + 2]]
    is_keeper = core in keeper
    noff = 0
    if is_keeper:
        here = [k for k in keeper if topo.chip(k) == topo.chip(core)]
        got = len(_split(topo, cores[r], here)[core])
        for q in (g.sync, g.scalar, g.vector):
            q.wait_ge(sem.parl, got)
        for j in range(1, 128 // Q):
            q = g.sync if j % 2 else g.scalar
            q.dma_start(T.parl[j * Q:(j + 1) * Q, :], T.parl[0:Q, :]).then_inc(sem.rep, 16)
        g.vector.wait_ge(sem.rep, 16 * (128 // Q - 1))
        n1 = N - 1 - r
        for e in range(W):
            if n1:
                g.vector.tensor_scalar(T.offl[:, e:n1 * W:W], T.parl[:, r + 1:N], W, e,
                                       AluOpType.mult, AluOpType.add).then_inc(sem.off, 1)
                noff += 1
            g.vector.tensor_scalar(T.offl[:, n1 * W + e:N * W:W], T.parl[:, 0:r + 1], W, e,
                                   AluOpType.mult, AluOpType.add).then_inc(sem.off, 1)
            noff += 1
    g.wait_ge(sem.hb, len(_split(topo, cores[r], pair)[core]))
    sent += _send(g, topo, core,
                  [(keeper[m], T.hb[:, j * BW:(j + 1) * BW], T.win[:, r * BW:(r + 1) * BW], sem.win)
                   for j, m in enumerate(ms)], sem.loc, together=True)
    if is_keeper:
        m = keeper.index(core)
        want = 0
        for rr in range(N):
            for h, hms in carry[rr]:
                if m in hms:
                    want += len(_split(topo, h, [keeper[x] for x in hms], True)[core])
        for q in (g.vector, g.scalar):
            q.wait_ge(sem.off, noff)
            q.wait_ge(sem.win, want)
        order = _order(r)
        waves = [(0, H), (H, N)]
        for w, (lo, hi) in enumerate(waves):
            a, z = lo * W, hi * W
            mid = (a + z) // 2
            g.vector.tensor_copy(T.gat[:, a * B:mid * B],
                                 T.win[:, 0:N * BW].indirect(T.offl[:, a:mid])).then_inc(sem["g%d" % w], 1)
            g.scalar.activation(T.gat[:, mid * B:z * B],
                                T.win[:, 0:N * BW].indirect(T.offl[:, mid:z]), copy).then_inc(sem["g%d" % w], 1)
        for w, (lo, hi) in enumerate(waves):
            g.wait_ge(sem["g%d" % w], 2)
            sent += _send(g, topo, core,
                          [(cores[order[p]], T.gat[:, p * BW:(p + 1) * BW], T.land[:, m * BW:(m + 1) * BW], sem.land)
                           for p in range(lo, hi)], sem.loc)
    g.wait_ge(sem.loc, sent)
